import numpy as np
import ml_dtypes


def mxq(x, axis, fmt="e4m3"):
    dtype, down = {"e4m3": (ml_dtypes.float8_e4m3fn, 7), "e5m2": (ml_dtypes.float8_e5m2, 14)}[fmt]
    v = np.moveaxis(np.asarray(x, np.float32).astype(ml_dtypes.bfloat16).astype(np.float64), axis, -1)
    blocks = v.reshape(v.shape[:-1] + (-1, 32))
    amax = np.abs(blocks).max(-1, keepdims=True)
    byte = np.maximum(np.where(amax > 0, np.frexp(amax)[1] - 1 + 127, 0) - down, 1)
    scale = np.exp2(byte - 127.0)
    codes = (blocks / scale).astype(np.float32).astype(dtype).astype(np.float64)
    return np.moveaxis((codes * scale).reshape(v.shape), -1, axis)


WIDE = False


def mx_kscale(k):
    if not WIDE:
        return np.ones(k)
    levels = np.array([10, -10, 5, -5, 0])
    if k % 512:
        return np.exp2(np.random.permutation(np.resize(levels, k // 32))).repeat(32)
    a = np.empty((k // 512, 16))
    for p in range(k // 512):
        a[p, :8] = np.random.permutation(np.resize(levels, 8))
        for g in range(8):
            far = levels[np.abs(levels - a[p, g]) >= 10]
            a[p, g + 8] = far[np.random.randint(len(far))]
    return np.exp2(a.ravel()).repeat(32)


def f64(x):
    return np.asarray(x).astype(np.float64)


def striped(idx):
    return np.tile(idx.reshape(-1, 16).T, (8, 1)).astype(np.uint16)


def unstriped(offs):
    return offs[:16].T.reshape(-1).astype(np.int64)


def pack_weight(w):
    k, n = w.shape
    w = f64(np.asarray(w, np.float32).astype(ml_dtypes.bfloat16)).reshape(k // 32, 32, n)
    amax = np.abs(w).max(1)
    byte = np.clip(np.where(amax > 0, np.frexp(amax)[1] - 1 + 127 - 7, 1), 1, 254)
    scaled = (w * np.exp2(127.0 - byte)[:, None, :]).reshape(k, n).astype(np.float32)
    words = np.ascontiguousarray(scaled.reshape(k // 512, 128, 4, n).transpose(0, 1, 3, 2)).astype(ml_dtypes.float8_e4m3fn).view(np.uint8)
    return words, np.ascontiguousarray(byte.astype(np.uint8).reshape(k // 512, 16, n))


def unpack_weight(words, scales):
    g, p, n, _ = words.shape
    vals = np.ascontiguousarray(words).view(ml_dtypes.float8_e4m3fn).astype(np.float64) * np.repeat(np.exp2(scales.astype(np.float64) - 127.0), 8, axis=1)[..., None]
    return vals.transpose(0, 1, 3, 2).reshape(g * 512, n)


def planes(y):
    n, m = y.shape
    v = y.astype(np.float32).astype(ml_dtypes.bfloat16).astype(np.float64).reshape(n // 32, 32, m)
    top = np.abs(v).max(1)
    byte = np.clip(np.where(top > 0, np.frexp(top)[1] - 1 + 127 - 7, 1), 1, 254)
    codes = (v * np.exp2(127.0 - byte)[:, None, :]).reshape(n, m).astype(np.float32).astype(ml_dtypes.float8_e4m3fn).view(np.uint8)
    words = codes.reshape(n // 512, 128, 4, m).transpose(0, 1, 3, 2)
    return np.ascontiguousarray(words), np.ascontiguousarray(byte.astype(np.uint8).reshape(n // 512, 16, m))


K, T, S, N, H, W, U = 512, 1024, 512, 512, 512, 1024, 1024


def setup_inputs():
    n = np.random.standard_normal
    s = mx_kscale(K)[:, None]
    u = mx_kscale(H)
    packed_xT = pack_weight(n((K, T)) * s)
    packed_eT = pack_weight(n((K, W)) * s)
    return {
        "x_words": packed_xT[0],
        "x_scales": packed_xT[1],
        "w1": (n((K, N)) / np.sqrt(K) / s).astype(np.float32),
        "e_words": packed_eT[0],
        "e_scales": packed_eT[1],
        "w2": (n((K, N)) / np.sqrt(K) / s).astype(np.float32),
        "unit": (np.random.uniform(0.6, 1.4, (H, 1)) * u[:, None]).astype(np.float32),
        "w3": (n((H, N)) / np.sqrt(H) / u[:, None]).astype(np.float32),
        "offs": striped(np.random.permutation(T)[:S]),
        "har": striped(np.random.permutation(W)[:S]),
        "nt": striped(np.random.permutation(np.concatenate([np.arange(S), np.random.randint(0, S, U - S)]))),
        "h1": striped(np.random.permutation(np.concatenate([np.arange(S), np.random.randint(0, S, U - S)]))),
        "h2": striped(np.random.permutation(np.concatenate([np.arange(S), np.random.randint(0, S, U - S)]))),
    }


def reference(x_words, x_scales, w1, e_words, e_scales, w2, unit, w3, offs, har, nt, h1, h2):
    xq = unpack_weight(x_words, x_scales)[:, unstriped(offs)]
    y = mxq(f64(w1), 0, "e4m3").T @ xq
    y_1 = y[:, unstriped(nt)]
    e_har = unpack_weight(e_words, e_scales)[:, unstriped(har)]
    ye = mxq(f64(w2), 0, "e4m3").T @ e_har
    e_1 = ye[:, unstriped(h1)]
    sum_ = y_1 + e_1
    e_2 = ye[:, unstriped(h2)]
    hid = f64(unit) * (sum_ / (np.abs(e_2) + 0.7))
    out_0 = mxq(f64(w3), 0, "e4m3").T @ mxq(hid, 0, "e4m3")
    return (out_0,) + planes(out_0)

@@ -1,0 +1,255 @@
+from contextlib import ExitStack
+
+import concourse.mybir as mybir
+
+K, T, S, H, N, U = 512, 1024, 512, 512, 512, 1024
+FLOPS = 2 * K * H * S * 2 + 2 * H * N * U
+
+F32 = mybir.dt.float32
+BF16 = mybir.dt.bfloat16
+I32 = mybir.dt.int32
+U32 = mybir.dt.uint32
+U16 = mybir.dt.uint16
+U8 = mybir.dt.uint8
+FP8X4 = mybir.dt.float8_e4m3fn_x4
+ACT = mybir.ActivationFunctionType
+ALU = mybir.AluOpType
+
+P = 128
+PACK = 4
+UNIT = 128
+CHUNKS = (256, 256, 256, 128, 128)
+SCALAR_ROUNDS = (0, 1, 2, 3, 4)
+SCALAR_FETCHES = (3, 4)
+
+
+def tile_picked_yharmon_rel_po_kernel(
+    tc, x_words, x_scales, w1, e_words, e_scales, w2, unit, w3, offs, har, nt, h1, h2, out_0, out_1, out_2
+):
+    nc = tc.nc
+    with ExitStack() as ctx:
+        keep = ctx.enter_context(tc.tile_pool(name="keep", bufs=1))
+        psum = ctx.enter_context(tc.psum_pool(name="psum", bufs=1))
+
+        def load_list(name, src):
+            tile = keep.tile(list(src.shape), U16, name=name)
+            nc.sync.dma_start(tile[:], src)
+            return tile
+
+        def load_scales(name, src):
+            tile = keep.tile([P, T], U8, name=name, align_bytes=64)
+            nc.vector.memset(tile[:].bitcast(I32), 0)
+            for q in range(4):
+                nc.sync.dma_start(tile[32 * q : 32 * q + 4, :].bitcast(I32), src[0, 4 * q : 4 * q + 4, :].bitcast(I32))
+            return tile
+
+        def load_words(name, src):
+            tile = keep.tile([P, T], I32, name=name, align_bytes=64)
+            nc.sync.dma_start(tile[:], src[0].rearrange("p c r -> p (c r)").bitcast(I32))
+            return tile
+
+        def load_weight(name, src, parts):
+            width = 512 // parts
+            tiles = []
+            for a in range(parts):
+                tile = keep.tile([P, PACK, width], F32, name=f"{name}_raw{a}", align_bytes=64)
+                nc.sync.dma_start(tile[:], src[:, a * width : (a + 1) * width].rearrange("(p j) c -> p j c", j=PACK))
+                tiles.append(tile)
+            return tiles
+
+        def pick(name, words, scales, offsets):
+            codes = keep.tile([P, S], U32, name=f"{name}_codes", align_bytes=64)
+            plane = keep.tile([P, S], U8, name=f"{name}_plane", align_bytes=64)
+            nc.vector.tensor_copy(codes[:], words[:].bitcast(U32).indirect(offsets[:]))
+            nc.vector.tensor_copy(plane[:], scales[:].indirect(offsets[:]))
+            return codes, plane
+
+        def grouped_weight(name):
+            return [keep.tile([P, 2, P, PACK], BF16, name=f"{name}_bf{h}", align_bytes=64) for h in range(2)]
+
+        def round_weight(copy, grouped, raw, a, h):
+            ms = P // len(raw)
+            copy(
+                grouped[h][:, :, a * ms : (a + 1) * ms, :].rearrange("p t m j -> p m j t"),
+                raw[a][:].rearrange("p j (m t) -> p m j t", t=PACK)[:, :, :, 2 * h : 2 * h + 2],
+            )
+
+        def quantise_weight(name, grouped, h):
+            codes = keep.tile([P, 2 * P], U32, name=f"{name}_codes{h}", align_bytes=64)
+            plane = keep.tile([P, 2 * P], U8, name=f"{name}_plane{h}", align_bytes=64)
+            nc.vector.quantize_mx(codes[:].bitcast(FP8X4), plane[:], grouped[h][:].rearrange("p t m j -> p (t m j)"))
+            return codes, plane
+
+        def product(dst, weight, t, codes, plane):
+            w_codes, w_plane = weight[t // 2]
+            cols = slice((t % 2) * P, (t % 2 + 1) * P)
+            nc.tensor.matmul_mx(
+                dst, lhsT=w_codes[:, cols].bitcast(FP8X4), lhsT_scale=w_plane[:, cols],
+                rhs=codes.bitcast(FP8X4), rhs_scale=plane, start=True, stop=True,
+            )
+
+        har_t = load_list("har_t", har)
+        e_sc = load_scales("e_sc", e_scales)
+        e_w = load_words("e_w", e_words)
+        w2_raw = load_weight("w2", w2, 2)
+        offs_t = load_list("offs_t", offs)
+        x_sc = load_scales("x_sc", x_scales)
+        x_w = load_words("x_w", x_words)
+        unit_t = keep.tile([P, PACK], F32, name="unit_t")
+        nc.sync.dma_start(unit_t[:], unit.rearrange("(p t) o -> p (t o)", t=PACK))
+        h1_t = load_list("h1_t", h1)
+        w1_raw = load_weight("w1", w1, 2)
+        nt_t = load_list("nt_t", nt)
+        h2_t = load_list("h2_t", h2)
+        w3_raw = load_weight("w3", w3, 1)
+
+        e_codes, e_plane = pick("e", e_w, e_sc, har_t)
+        w2_bf = grouped_weight("w2")
+        round_weight(nc.scalar.copy, w2_bf, w2_raw, 0, 0)
+        round_weight(nc.scalar.copy, w2_bf, w2_raw, 0, 1)
+        round_weight(nc.scalar.copy, w2_bf, w2_raw, 1, 0)
+        round_weight(nc.vector.tensor_copy, w2_bf, w2_raw, 1, 1)
+        w2_q = [quantise_weight("w2", w2_bf, h) for h in range(2)]
+        ye_ps, ye, mag = [], [], []
+        for t in range(PACK):
+            bank = psum.tile([P, S], F32, name=f"ye_ps{t}", tag=f"bank{t}")
+            product(bank[:], w2_q, t, e_codes[:], e_plane[:])
+            ye_ps.append(bank)
+        for t in range(PACK):
+            tile = keep.tile([P, S], F32, name=f"ye{t}")
+            nc.scalar.activation(tile[:], ye_ps[t][:], ACT.Copy, scale=unit_t[:, t : t + 1])
+            ye.append(tile)
+
+        x_codes, x_plane = pick("x", x_w, x_sc, offs_t)
+        w1_bf = grouped_weight("w1")
+        for a in range(2):
+            for h in range(2):
+                round_weight(nc.vector.tensor_copy, w1_bf, w1_raw, a, h)
+        w1_q = [quantise_weight("w1", w1_bf, h) for h in range(2)]
+        y_ps, y = [], []
+        for t in range(PACK):
+            bank = psum.tile([P, S], F32, name=f"y_ps{t}", tag=f"bank{PACK + t}")
+            product(bank[:], w1_q, t, x_codes[:], x_plane[:])
+            y_ps.append(bank)
+
+        starts = [sum(CHUNKS[:c]) for c in range(len(CHUNKS))]
+
+        def entries(tile, c):
+            return tile[:, starts[c] // 16 : (starts[c] + CHUNKS[c]) // 16]
+
+        first, sums, hid, hid_bf, hid_q, res, res_bf = {}, {}, {}, {}, {}, {}, {}
+
+        def fetch_first(c, t):
+            first[c, t] = keep.tile([P, CHUNKS[c]], F32, name=f"first{c}_{t}", tag=f"first{t}")
+            nc.scalar.activation(first[c, t][:], ye[t][:].indirect(entries(h1_t, c)), ACT.Copy)
+
+        root, inv = {}, {}
+        for t in range(PACK):
+            fetch_first(0, t)
+        for t in range(PACK):
+            tile = keep.tile([P, S], F32, name=f"y{t}")
+            nc.vector.tensor_scalar(tile[:], y_ps[t][:], unit_t[:, t : t + 1], None, ALU.mult)
+            y.append(tile)
+        for pair in ((0, 1), (2, 3)):
+            for t in pair:
+                tile = keep.tile([P, S], F32, name=f"mag{t}")
+                nc.scalar.activation(tile[:], ye_ps[t][:], ACT.Abs)
+                mag.append(tile)
+            for t in pair:
+                root[t] = keep.tile([P, S], F32, name=f"root{t}")
+                nc.scalar.activation(root[t][:], mag[t][:], ACT.Abs_reciprocal_sqrt, bias=0.7)
+            for t in pair:
+                inv[t] = keep.tile([P, S], F32, name=f"inv{t}")
+                nc.scalar.activation(inv[t][:], root[t][:], ACT.Square)
+        w3_bf = grouped_weight("w3")
+
+        def add_note(c, t):
+            if t == 0:
+                sums[c] = keep.tile([P, PACK, CHUNKS[c]], F32, name=f"sum{c}")
+            nc.vector.tensor_tensor(sums[c][:, t, :], y[t][:].indirect(entries(nt_t, c)), first[c, t][:], ALU.add)
+
+        def divide(c, t):
+            if t == 0:
+                hid[c] = keep.tile([P, PACK, CHUNKS[c]], F32, name=f"hid{c}", tag=f"hid{c % 2}")
+            if c in SCALAR_FETCHES:
+                nc.scalar.activation(hid[c][:, t, :], inv[t][:].indirect(entries(h2_t, c)), ACT.Copy)
+            else:
+                nc.vector.tensor_tensor(hid[c][:, t, :], inv[t][:].indirect(entries(h2_t, c)), sums[c][:, t, :], ALU.mult)
+
+        def by_column(ap):
+            return ap.rearrange("p (c i) t -> p c t i", i=2)
+
+        def by_slot(ap):
+            return ap.rearrange("p t (c i) -> p c t i", i=2)
+
+        def interleave(copy, dst, src):
+            copy(by_column(dst), by_slot(src))
+
+        def round_hid(c):
+            hid_bf[c] = keep.tile([P, CHUNKS[c], PACK], BF16, name=f"hid_bf{c}", align_bytes=64)
+            if c in SCALAR_FETCHES:
+                nc.vector.tensor_tensor(by_column(hid_bf[c][:]), by_slot(hid[c][:]), by_slot(sums[c][:]), ALU.mult)
+            else:
+                interleave(nc.vector.tensor_copy, hid_bf[c][:], hid[c][:])
+
+        out_plane = keep.tile([P, U], U8, name="out_plane", align_bytes=64)
+        out_rows = out_0.rearrange("(p t) r -> p t r", t=PACK)
+        out_words = out_1[0].rearrange("p c r -> p (c r)").bitcast(I32)
+        w3_q = []
+
+        def voices(c):
+            width = CHUNKS[c]
+            codes = keep.tile([P, width], U32, name=f"hid_codes{c}", align_bytes=64)
+            plane = keep.tile([P, width], U8, name=f"hid_plane{c}", align_bytes=64)
+            nc.vector.quantize_mx(codes[:].bitcast(FP8X4), plane[:], hid_bf[c][:].rearrange("p n t -> p (n t)"))
+            res[c] = keep.tile([P, PACK, width], F32, name=f"res{c}")
+            res_bf[c] = keep.tile([P, width, PACK], BF16, name=f"res_bf{c}", align_bytes=64)
+            for u in range(width // UNIT):
+                cols = slice(u * UNIT, (u + 1) * UNIT)
+                g = starts[c] // UNIT + u
+                bank = psum.tile([P, PACK, UNIT], F32, name=f"out_ps{g}", tag=f"bank{g}")
+                for t in range(PACK):
+                    product(bank[:, t, :], w3_q, t, codes[:, cols], plane[:, cols])
+                if c in SCALAR_ROUNDS:
+                    interleave(nc.scalar.copy, res_bf[c][:, cols, :], bank[:])
+                nc.scalar.copy(res[c][:, :, cols], bank[:])
+            nc.sync.dma_start(out_rows[:, :, starts[c] : starts[c] + width], res[c][:])
+
+        def round_result(c):
+            if c not in SCALAR_ROUNDS:
+                interleave(nc.vector.tensor_copy, res_bf[c][:], res[c][:])
+
+        def hand_on(c):
+            cols = slice(starts[c], starts[c] + CHUNKS[c])
+            codes = keep.tile([P, CHUNKS[c]], I32, name=f"out_codes{c}", align_bytes=64)
+            nc.vector.quantize_mx(codes[:].bitcast(FP8X4), out_plane[:, cols], res_bf[c][:].rearrange("p n t -> p (n t)"))
+            nc.sync.dma_start(out_words[:, cols], codes[:])
+
+        last = len(CHUNKS) - 1
+        for c in range(len(CHUNKS)):
+            add_note(c, 0)
+            if c > 0:
+                voices(c - 1)
+            for t in range(1, PACK):
+                add_note(c, t)
+            if c == 0:
+                for h in range(2):
+                    round_weight(nc.vector.tensor_copy, w3_bf, w3_raw, 0, h)
+                for h in range(2):
+                    w3_q.append(quantise_weight("w3", w3_bf, h))
+            if c + 1 <= last:
+                for t in range(PACK):
+                    fetch_first(c + 1, t)
+            for t in range(PACK):
+                divide(c, t)
+            if c > 0:
+                round_result(c - 1)
+            round_hid(c)
+            if c > 0:
+                hand_on(c - 1)
+        voices(last)
+        round_result(last)
+        hand_on(last)
+        for q in range(4):
+            queue = nc.sync if q % 2 else nc.scalar
+            queue.dma_start(out_2[0, 4 * q : 4 * q + 4, :].bitcast(I32), out_plane[32 * q : 32 * q + 4, :].bitcast(I32))

@@ -18,9 +18,8 @@ ALU = mybir.AluOpType
 P = 128
 PACK = 4
 UNIT = 128
-CHUNKS = (256, 256, 256, 128, 128)
-SCALAR_ROUNDS = (0, 1, 2, 3, 4)
-SCALAR_FETCHES = (3, 4)
+CHUNKS = (384, 384, 256)
+SCALAR_FETCHES = (1, 2)
 
 
 def tile_picked_yharmon_rel_po_kernel(
@@ -48,14 +47,11 @@ def tile_picked_yharmon_rel_po_kernel(
             nc.sync.dma_start(tile[:], src[0].rearrange("p c r -> p (c r)").bitcast(I32))
             return tile
 
-        def load_weight(name, src, parts):
+        def load_weight(name, src, a, parts):
             width = 512 // parts
-            tiles = []
-            for a in range(parts):
-                tile = keep.tile([P, PACK, width], F32, name=f"{name}_raw{a}", align_bytes=64)
-                nc.sync.dma_start(tile[:], src[:, a * width : (a + 1) * width].rearrange("(p j) c -> p j c", j=PACK))
-                tiles.append(tile)
-            return tiles
+            tile = keep.tile([P, PACK, width], F32, name=f"{name}_raw{a}", align_bytes=64)
+            nc.sync.dma_start(tile[:], src[:, a * width : (a + 1) * width].rearrange("(p j) c -> p j c", j=PACK))
+            return tile
 
         def pick(name, words, scales, offsets):
             codes = keep.tile([P, S], U32, name=f"{name}_codes", align_bytes=64)
@@ -89,20 +85,25 @@ def tile_picked_yharmon_rel_po_kernel(
             )
 
         har_t = load_list("har_t", har)
-        e_sc = load_scales("e_sc", e_scales)
         e_w = load_words("e_w", e_words)
-        w2_raw = load_weight("w2", w2, 2)
+        e_sc = load_scales("e_sc", e_scales)
+        w2_raw = [load_weight("w2", w2, a, 2) for a in range(2)]
         offs_t = load_list("offs_t", offs)
-        x_sc = load_scales("x_sc", x_scales)
         x_w = load_words("x_w", x_words)
         unit_t = keep.tile([P, PACK], F32, name="unit_t")
         nc.sync.dma_start(unit_t[:], unit.rearrange("(p t) o -> p (t o)", t=PACK))
         h1_t = load_list("h1_t", h1)
-        w1_raw = load_weight("w1", w1, 2)
+        w1_raw = [load_weight("w1", w1, 0, 2)]
+        x_sc = load_scales("x_sc", x_scales)
+        w1_raw.append(load_weight("w1", w1, 1, 2))
         nt_t = load_list("nt_t", nt)
         h2_t = load_list("h2_t", h2)
-        w3_raw = load_weight("w3", w3, 1)
+        w3_raw = [load_weight("w3", w3, 0, 1)]
 
+        warm = keep.tile([P, 2], F32, name="warm")
+        nc.gpsimd.memset(warm[:, 0:1], 1.0)
+        warm_out = keep.tile([P, 1], F32, name="warm_out")
+        nc.scalar.activation(warm_out[:], warm[:, 0:1], ACT.Abs_reciprocal_sqrt, bias=0.7)
         e_codes, e_plane = pick("e", e_w, e_sc, har_t)
         w2_bf = grouped_weight("w2")
         round_weight(nc.scalar.copy, w2_bf, w2_raw, 0, 0)
@@ -110,7 +111,7 @@ def tile_picked_yharmon_rel_po_kernel(
         round_weight(nc.scalar.copy, w2_bf, w2_raw, 1, 0)
         round_weight(nc.vector.tensor_copy, w2_bf, w2_raw, 1, 1)
         w2_q = [quantise_weight("w2", w2_bf, h) for h in range(2)]
-        ye_ps, ye, mag = [], [], []
+        ye_ps, ye = [], []
         for t in range(PACK):
             bank = psum.tile([P, S], F32, name=f"ye_ps{t}", tag=f"bank{t}")
             product(bank[:], w2_q, t, e_codes[:], e_plane[:])
@@ -140,37 +141,35 @@ def tile_picked_yharmon_rel_po_kernel(
         first, sums, hid, hid_bf, hid_q, res, res_bf = {}, {}, {}, {}, {}, {}, {}
 
         def fetch_first(c, t):
-            first[c, t] = keep.tile([P, CHUNKS[c]], F32, name=f"first{c}_{t}", tag=f"first{t}")
+            first[c, t] = keep.tile([P, CHUNKS[c]], F32, name=f"first{c}_{t}", tag=f"first{c % 2}_{t}")
             nc.scalar.activation(first[c, t][:], ye[t][:].indirect(entries(h1_t, c)), ACT.Copy)
 
-        root, inv = {}, {}
+        inv = {}
         for t in range(PACK):
             fetch_first(0, t)
         for t in range(PACK):
             tile = keep.tile([P, S], F32, name=f"y{t}")
             nc.vector.tensor_scalar(tile[:], y_ps[t][:], unit_t[:, t : t + 1], None, ALU.mult)
             y.append(tile)
-        for pair in ((0, 1), (2, 3)):
-            for t in pair:
-                tile = keep.tile([P, S], F32, name=f"mag{t}")
-                nc.scalar.activation(tile[:], ye_ps[t][:], ACT.Abs)
-                mag.append(tile)
-            for t in pair:
-                root[t] = keep.tile([P, S], F32, name=f"root{t}")
-                nc.scalar.activation(root[t][:], mag[t][:], ACT.Abs_reciprocal_sqrt, bias=0.7)
-            for t in pair:
-                inv[t] = keep.tile([P, S], F32, name=f"inv{t}")
-                nc.scalar.activation(inv[t][:], root[t][:], ACT.Square)
+        for h in range(2):
+            mag = keep.tile([P, 2, S], F32, name=f"mag{h}")
+            root = keep.tile([P, 2, S], F32, name=f"root{h}")
+            for i in range(2):
+                nc.scalar.activation(mag[:, i, :], ye_ps[2 * h + i][:], ACT.Abs)
+            nc.scalar.activation(root[:], mag[:], ACT.Abs_reciprocal_sqrt, bias=0.7)
+            for i in range(2):
+                inv[2 * h + i] = keep.tile([P, S], F32, name=f"inv{2 * h + i}")
+                nc.scalar.activation(inv[2 * h + i][:], root[:, i, :], ACT.Square)
         w3_bf = grouped_weight("w3")
 
         def add_note(c, t):
             if t == 0:
-                sums[c] = keep.tile([P, PACK, CHUNKS[c]], F32, name=f"sum{c}")
+                sums[c] = keep.tile([P, PACK, CHUNKS[c]], F32, name=f"sum{c}", tag=f"sum{c}", align_bytes=64)
             nc.vector.tensor_tensor(sums[c][:, t, :], y[t][:].indirect(entries(nt_t, c)), first[c, t][:], ALU.add)
 
         def divide(c, t):
             if t == 0:
-                hid[c] = keep.tile([P, PACK, CHUNKS[c]], F32, name=f"hid{c}", tag=f"hid{c % 2}")
+                hid[c] = keep.tile([P, PACK, CHUNKS[c]], F32, name=f"hid{c}", tag=f"hid{c}", align_bytes=64)
             if c in SCALAR_FETCHES:
                 nc.scalar.activation(hid[c][:, t, :], inv[t][:].indirect(entries(h2_t, c)), ACT.Copy)
             else:
@@ -185,47 +184,56 @@ def tile_picked_yharmon_rel_po_kernel(
         def interleave(copy, dst, src):
             copy(by_column(dst), by_slot(src))
 
-        def round_hid(c):
-            hid_bf[c] = keep.tile([P, CHUNKS[c], PACK], BF16, name=f"hid_bf{c}", align_bytes=64)
+        last = len(CHUNKS) - 1
+        groups = [(c, 0, CHUNKS[c]) for c in range(last)] + [(last, a, UNIT) for a in range(0, CHUNKS[last], UNIT)]
+
+        def round_hid(k):
+            c, a, width = groups[k]
+            cols = slice(a, a + width)
+            hid_bf[k] = keep.tile([P, width, PACK], BF16, name=f"hid_bf{k}", align_bytes=64)
             if c in SCALAR_FETCHES:
-                nc.vector.tensor_tensor(by_column(hid_bf[c][:]), by_slot(hid[c][:]), by_slot(sums[c][:]), ALU.mult)
+                nc.vector.tensor_tensor(
+                    by_column(hid_bf[k][:]), by_slot(hid[c][:, :, cols]), by_slot(sums[c][:, :, cols]), ALU.mult
+                )
             else:
-                interleave(nc.vector.tensor_copy, hid_bf[c][:], hid[c][:])
+                interleave(nc.vector.tensor_copy, hid_bf[k][:], hid[c][:, :, cols])
 
         out_plane = keep.tile([P, U], U8, name="out_plane", align_bytes=64)
         out_rows = out_0.rearrange("(p t) r -> p t r", t=PACK)
         out_words = out_1[0].rearrange("p c r -> p (c r)").bitcast(I32)
         w3_q = []
 
-        def voices(c):
-            width = CHUNKS[c]
-            codes = keep.tile([P, width], U32, name=f"hid_codes{c}", align_bytes=64)
-            plane = keep.tile([P, width], U8, name=f"hid_plane{c}", align_bytes=64)
-            nc.vector.quantize_mx(codes[:].bitcast(FP8X4), plane[:], hid_bf[c][:].rearrange("p n t -> p (n t)"))
-            res[c] = keep.tile([P, PACK, width], F32, name=f"res{c}")
-            res_bf[c] = keep.tile([P, width, PACK], BF16, name=f"res_bf{c}", align_bytes=64)
+        def voices(k):
+            c, a, width = groups[k]
+            start = starts[c] + a
+            codes = keep.tile([P, width], U32, name=f"hid_codes{k}", tag=f"hid{k + 2}", align_bytes=64)
+            plane = keep.tile([P, width], U8, name=f"hid_plane{k}", align_bytes=64)
+            nc.vector.quantize_mx(codes[:].bitcast(FP8X4), plane[:], hid_bf[k][:].rearrange("p n t -> p (n t)"))
+            res[k] = keep.tile([P, PACK, width], F32, name=f"res{k}")
+            if c == last:
+                res_bf[k] = keep.tile([P, width, PACK], BF16, name=f"res_bf{k}", align_bytes=64)
             for u in range(width // UNIT):
                 cols = slice(u * UNIT, (u + 1) * UNIT)
-                g = starts[c] // UNIT + u
+                g = start // UNIT + u
                 bank = psum.tile([P, PACK, UNIT], F32, name=f"out_ps{g}", tag=f"bank{g}")
                 for t in range(PACK):
                     product(bank[:, t, :], w3_q, t, codes[:, cols], plane[:, cols])
-                if c in SCALAR_ROUNDS:
-                    interleave(nc.scalar.copy, res_bf[c][:, cols, :], bank[:])
-                nc.scalar.copy(res[c][:, :, cols], bank[:])
-            nc.sync.dma_start(out_rows[:, :, starts[c] : starts[c] + width], res[c][:])
+                if c == last:
+                    interleave(nc.scalar.copy, res_bf[k][:, cols, :], bank[:])
+                nc.scalar.copy(res[k][:, :, cols], bank[:])
+            nc.sync.dma_start(out_rows[:, :, start : start + width], res[k][:])
 
-        def round_result(c):
-            if c not in SCALAR_ROUNDS:
-                interleave(nc.vector.tensor_copy, res_bf[c][:], res[c][:])
+        def round_result(k):
+            res_bf[k] = keep.tile([P, groups[k][2], PACK], BF16, name=f"res_bf{k}", tag=f"sum{k + 1}", align_bytes=64)
+            interleave(nc.vector.tensor_copy, res_bf[k][:], res[k][:])
 
-        def hand_on(c):
-            cols = slice(starts[c], starts[c] + CHUNKS[c])
-            codes = keep.tile([P, CHUNKS[c]], I32, name=f"out_codes{c}", align_bytes=64)
-            nc.vector.quantize_mx(codes[:].bitcast(FP8X4), out_plane[:, cols], res_bf[c][:].rearrange("p n t -> p (n t)"))
+        def hand_on(k):
+            c, a, width = groups[k]
+            cols = slice(starts[c] + a, starts[c] + a + width)
+            codes = keep.tile([P, width], I32, name=f"out_codes{k}", align_bytes=64)
+            nc.vector.quantize_mx(codes[:].bitcast(FP8X4), out_plane[:, cols], res_bf[k][:].rearrange("p n t -> p (n t)"))
             nc.sync.dma_start(out_words[:, cols], codes[:])
 
-        last = len(CHUNKS) - 1
         for c in range(len(CHUNKS)):
             add_note(c, 0)
             if c > 0:
@@ -237,19 +245,22 @@ def tile_picked_yharmon_rel_po_kernel(
                     round_weight(nc.vector.tensor_copy, w3_bf, w3_raw, 0, h)
                 for h in range(2):
                     w3_q.append(quantise_weight("w3", w3_bf, h))
-            if c + 1 <= last:
-                for t in range(PACK):
-                    fetch_first(c + 1, t)
             for t in range(PACK):
                 divide(c, t)
-            if c > 0:
-                round_result(c - 1)
+            if c < last:
+                for t in range(PACK):
+                    fetch_first(c + 1, t)
             round_hid(c)
-            if c > 0:
+            if 0 < c < last:
+                round_result(c - 1)
                 hand_on(c - 1)
-        voices(last)
-        round_result(last)
-        hand_on(last)
+        for k in range(last + 1, len(groups)):
+            round_hid(k)
+        for k in range(last, len(groups)):
+            voices(k)
+        round_result(last - 1)
+        for k in range(last - 1, len(groups)):
+            hand_on(k)
         for q in range(4):
             queue = nc.sync if q % 2 else nc.scalar
             queue.dma_start(out_2[0, 4 * q : 4 * q + 4, :].bitcast(I32), out_plane[32 * q : 32 * q + 4, :].bitcast(I32))

@@ -47,10 +47,9 @@ def tile_picked_yharmon_rel_po_kernel(
             nc.sync.dma_start(tile[:], src[0].rearrange("p c r -> p (c r)").bitcast(I32))
             return tile
 
-        def load_weight(name, src, a, parts):
-            width = 512 // parts
-            tile = keep.tile([P, PACK, width], F32, name=f"{name}_raw{a}", align_bytes=64)
-            nc.sync.dma_start(tile[:], src[:, a * width : (a + 1) * width].rearrange("(p j) c -> p j c", j=PACK))
+        def load_weight(name, src):
+            tile = keep.tile([P, PACK, 512], F32, name=f"{name}_raw", align_bytes=64)
+            nc.sync.dma_start(tile[:], src.rearrange("(p j) c -> p j c", j=PACK))
             return tile
 
         def pick(name, words, scales, offsets):
@@ -63,11 +62,10 @@ def tile_picked_yharmon_rel_po_kernel(
         def grouped_weight(name):
             return [keep.tile([P, 2, P, PACK], BF16, name=f"{name}_bf{h}", align_bytes=64) for h in range(2)]
 
-        def round_weight(copy, grouped, raw, a, h):
-            ms = P // len(raw)
+        def round_weight(copy, grouped, raw, h):
             copy(
-                grouped[h][:, :, a * ms : (a + 1) * ms, :].rearrange("p t m j -> p m j t"),
-                raw[a][:].rearrange("p j (m t) -> p m j t", t=PACK)[:, :, :, 2 * h : 2 * h + 2],
+                grouped[h][:].rearrange("p t m j -> p m j t"),
+                raw[:].rearrange("p j (m t) -> p m j t", t=PACK)[:, :, :, 2 * h : 2 * h + 2],
             )
 
         def quantise_weight(name, grouped, h):
@@ -87,18 +85,17 @@ def tile_picked_yharmon_rel_po_kernel(
         har_t = load_list("har_t", har)
         e_w = load_words("e_w", e_words)
         e_sc = load_scales("e_sc", e_scales)
-        w2_raw = [load_weight("w2", w2, a, 2) for a in range(2)]
+        w2_raw = load_weight("w2", w2)
         offs_t = load_list("offs_t", offs)
         x_w = load_words("x_w", x_words)
         unit_t = keep.tile([P, PACK], F32, name="unit_t")
         nc.sync.dma_start(unit_t[:], unit.rearrange("(p t) o -> p (t o)", t=PACK))
-        h1_t = load_list("h1_t", h1)
-        w1_raw = [load_weight("w1", w1, 0, 2)]
         x_sc = load_scales("x_sc", x_scales)
-        w1_raw.append(load_weight("w1", w1, 1, 2))
+        w1_raw = load_weight("w1", w1)
+        h1_t = load_list("h1_t", h1)
         nt_t = load_list("nt_t", nt)
         h2_t = load_list("h2_t", h2)
-        w3_raw = [load_weight("w3", w3, 0, 1)]
+        w3_raw = load_weight("w3", w3)
 
         warm = keep.tile([P, 2], F32, name="warm")
         nc.gpsimd.memset(warm[:, 0:1], 1.0)
@@ -106,10 +103,8 @@ def tile_picked_yharmon_rel_po_kernel(
         nc.scalar.activation(warm_out[:], warm[:, 0:1], ACT.Abs_reciprocal_sqrt, bias=0.7)
         e_codes, e_plane = pick("e", e_w, e_sc, har_t)
         w2_bf = grouped_weight("w2")
-        round_weight(nc.scalar.copy, w2_bf, w2_raw, 0, 0)
-        round_weight(nc.scalar.copy, w2_bf, w2_raw, 0, 1)
-        round_weight(nc.scalar.copy, w2_bf, w2_raw, 1, 0)
-        round_weight(nc.vector.tensor_copy, w2_bf, w2_raw, 1, 1)
+        round_weight(nc.vector.tensor_copy, w2_bf, w2_raw, 0)
+        round_weight(nc.scalar.copy, w2_bf, w2_raw, 1)
         w2_q = [quantise_weight("w2", w2_bf, h) for h in range(2)]
         ye_ps, ye = [], []
         for t in range(PACK):
@@ -123,9 +118,8 @@ def tile_picked_yharmon_rel_po_kernel(
 
         x_codes, x_plane = pick("x", x_w, x_sc, offs_t)
         w1_bf = grouped_weight("w1")
-        for a in range(2):
-            for h in range(2):
-                round_weight(nc.vector.tensor_copy, w1_bf, w1_raw, a, h)
+        for h in range(2):
+            round_weight(nc.vector.tensor_copy, w1_bf, w1_raw, h)
         w1_q = [quantise_weight("w1", w1_bf, h) for h in range(2)]
         y_ps, y = [], []
         for t in range(PACK):
@@ -220,19 +214,29 @@ def tile_picked_yharmon_rel_po_kernel(
                     product(bank[:, t, :], w3_q, t, codes[:, cols], plane[:, cols])
                 if c == last:
                     interleave(nc.scalar.copy, res_bf[k][:, cols, :], bank[:])
-                nc.scalar.copy(res[k][:, :, cols], bank[:])
+                if k == len(groups) - 1:
+                    nc.vector.tensor_copy(res[k][:, :, cols], bank[:])
+                else:
+                    nc.scalar.copy(res[k][:, :, cols], bank[:])
             nc.sync.dma_start(out_rows[:, :, start : start + width], res[k][:])
 
         def round_result(k):
             res_bf[k] = keep.tile([P, groups[k][2], PACK], BF16, name=f"res_bf{k}", tag=f"sum{k + 1}", align_bytes=64)
             interleave(nc.vector.tensor_copy, res_bf[k][:], res[k][:])
 
+        out_codes = {}
+
         def hand_on(k):
             c, a, width = groups[k]
-            cols = slice(starts[c] + a, starts[c] + a + width)
-            codes = keep.tile([P, width], I32, name=f"out_codes{k}", align_bytes=64)
-            nc.vector.quantize_mx(codes[:].bitcast(FP8X4), out_plane[:, cols], res_bf[k][:].rearrange("p n t -> p (n t)"))
-            nc.sync.dma_start(out_words[:, cols], codes[:])
+            if a == 0:
+                out_codes[c] = keep.tile([P, CHUNKS[c]], I32, name=f"out_codes{c}", align_bytes=64)
+            nc.vector.quantize_mx(
+                out_codes[c][:, a : a + width].bitcast(FP8X4),
+                out_plane[:, starts[c] + a : starts[c] + a + width],
+                res_bf[k][:].rearrange("p n t -> p (n t)"),
+            )
+            if a + width == CHUNKS[c]:
+                nc.sync.dma_start(out_words[:, starts[c] : starts[c] + CHUNKS[c]], out_codes[c][:])
 
         for c in range(len(CHUNKS)):
             add_note(c, 0)
@@ -242,7 +246,7 @@ def tile_picked_yharmon_rel_po_kernel(
                 add_note(c, t)
             if c == 0:
                 for h in range(2):
-                    round_weight(nc.vector.tensor_copy, w3_bf, w3_raw, 0, h)
+                    round_weight(nc.vector.tensor_copy, w3_bf, w3_raw, h)
                 for h in range(2):
                     w3_q.append(quantise_weight("w3", w3_bf, h))
             for t in range(PACK):

from contextlib import ExitStack

import concourse.mybir as mybir

K, T, S, H, N, U = 512, 1024, 512, 512, 512, 1024
FLOPS = 2 * K * H * S * 2 + 2 * H * N * U

F32 = mybir.dt.float32
BF16 = mybir.dt.bfloat16
I32 = mybir.dt.int32
U32 = mybir.dt.uint32
U16 = mybir.dt.uint16
U8 = mybir.dt.uint8
FP8X4 = mybir.dt.float8_e4m3fn_x4
ACT = mybir.ActivationFunctionType
ALU = mybir.AluOpType

P = 128
PACK = 4
UNIT = 128
CHUNKS = (384, 384, 256)
SCALAR_FETCHES = (1, 2)


def tile_picked_yharmon_rel_po_kernel(
    tc, x_words, x_scales, w1, e_words, e_scales, w2, unit, w3, offs, har, nt, h1, h2, out_0, out_1, out_2
):
    nc = tc.nc
    with ExitStack() as ctx:
        keep = ctx.enter_context(tc.tile_pool(name="keep", bufs=1))
        psum = ctx.enter_context(tc.psum_pool(name="psum", bufs=1))

        def load_list(name, src):
            tile = keep.tile(list(src.shape), U16, name=name)
            nc.sync.dma_start(tile[:], src)
            return tile

        def load_scales(name, src):
            tile = keep.tile([P, T], U8, name=name, align_bytes=64)
            nc.vector.memset(tile[:].bitcast(I32), 0)
            for q in range(4):
                nc.sync.dma_start(tile[32 * q : 32 * q + 4, :].bitcast(I32), src[0, 4 * q : 4 * q + 4, :].bitcast(I32))
            return tile

        def load_words(name, src):
            tile = keep.tile([P, T], I32, name=name, align_bytes=64)
            nc.sync.dma_start(tile[:], src[0].rearrange("p c r -> p (c r)").bitcast(I32))
            return tile

        def load_weight(name, src):
            tile = keep.tile([P, PACK, 512], F32, name=f"{name}_raw", align_bytes=64)
            nc.sync.dma_start(tile[:], src.rearrange("(p j) c -> p j c", j=PACK))
            return tile

        def pick(name, words, scales, offsets):
            codes = keep.tile([P, S], U32, name=f"{name}_codes", align_bytes=64)
            plane = keep.tile([P, S], U8, name=f"{name}_plane", align_bytes=64)
            nc.vector.tensor_copy(codes[:], words[:].bitcast(U32).indirect(offsets[:]))
            nc.vector.tensor_copy(plane[:], scales[:].indirect(offsets[:]))
            return codes, plane

        def grouped_weight(name):
            return [keep.tile([P, 2, P, PACK], BF16, name=f"{name}_bf{h}", align_bytes=64) for h in range(2)]

        def round_weight(copy, grouped, raw, h):
            copy(
                grouped[h][:].rearrange("p t m j -> p m j t"),
                raw[:].rearrange("p j (m t) -> p m j t", t=PACK)[:, :, :, 2 * h : 2 * h + 2],
            )

        def quantise_weight(name, grouped, h):
            codes = keep.tile([P, 2 * P], U32, name=f"{name}_codes{h}", align_bytes=64)
            plane = keep.tile([P, 2 * P], U8, name=f"{name}_plane{h}", align_bytes=64)
            nc.vector.quantize_mx(codes[:].bitcast(FP8X4), plane[:], grouped[h][:].rearrange("p t m j -> p (t m j)"))
            return codes, plane

        def product(dst, weight, t, codes, plane):
            w_codes, w_plane = weight[t // 2]
            cols = slice((t % 2) * P, (t % 2 + 1) * P)
            nc.tensor.matmul_mx(
                dst, lhsT=w_codes[:, cols].bitcast(FP8X4), lhsT_scale=w_plane[:, cols],
                rhs=codes.bitcast(FP8X4), rhs_scale=plane, start=True, stop=True,
            )

        har_t = load_list("har_t", har)
        e_w = load_words("e_w", e_words)
        e_sc = load_scales("e_sc", e_scales)
        w2_raw = load_weight("w2", w2)
        offs_t = load_list("offs_t", offs)
        x_w = load_words("x_w", x_words)
        unit_t = keep.tile([P, PACK], F32, name="unit_t")
        nc.sync.dma_start(unit_t[:], unit.rearrange("(p t) o -> p (t o)", t=PACK))
        x_sc = load_scales("x_sc", x_scales)
        w1_raw = load_weight("w1", w1)
        h1_t = load_list("h1_t", h1)
        nt_t = load_list("nt_t", nt)
        h2_t = load_list("h2_t", h2)
        w3_raw = load_weight("w3", w3)

        warm = keep.tile([P, 2], F32, name="warm")
        nc.gpsimd.memset(warm[:, 0:1], 1.0)
        warm_out = keep.tile([P, 1], F32, name="warm_out")
        nc.scalar.activation(warm_out[:], warm[:, 0:1], ACT.Abs_reciprocal_sqrt, bias=0.7)
        e_codes, e_plane = pick("e", e_w, e_sc, har_t)
        w2_bf = grouped_weight("w2")
        round_weight(nc.vector.tensor_copy, w2_bf, w2_raw, 0)
        round_weight(nc.scalar.copy, w2_bf, w2_raw, 1)
        w2_q = [quantise_weight("w2", w2_bf, h) for h in range(2)]
        ye_ps, ye = [], []
        for t in range(PACK):
            bank = psum.tile([P, S], F32, name=f"ye_ps{t}", tag=f"bank{t}")
            product(bank[:], w2_q, t, e_codes[:], e_plane[:])
            ye_ps.append(bank)
        for t in range(PACK):
            tile = keep.tile([P, S], F32, name=f"ye{t}")
            nc.scalar.activation(tile[:], ye_ps[t][:], ACT.Copy, scale=unit_t[:, t : t + 1])
            ye.append(tile)

        x_codes, x_plane = pick("x", x_w, x_sc, offs_t)
        w1_bf = grouped_weight("w1")
        for h in range(2):
            round_weight(nc.vector.tensor_copy, w1_bf, w1_raw, h)
        w1_q = [quantise_weight("w1", w1_bf, h) for h in range(2)]
        y_ps, y = [], []
        for t in range(PACK):
            bank = psum.tile([P, S], F32, name=f"y_ps{t}", tag=f"bank{PACK + t}")
            product(bank[:], w1_q, t, x_codes[:], x_plane[:])
            y_ps.append(bank)

        starts = [sum(CHUNKS[:c]) for c in range(len(CHUNKS))]

        def entries(tile, c):
            return tile[:, starts[c] // 16 : (starts[c] + CHUNKS[c]) // 16]

        first, sums, hid, hid_bf, hid_q, res, res_bf = {}, {}, {}, {}, {}, {}, {}

        def fetch_first(c, t):
            first[c, t] = keep.tile([P, CHUNKS[c]], F32, name=f"first{c}_{t}", tag=f"first{c % 2}_{t}")
            nc.scalar.activation(first[c, t][:], ye[t][:].indirect(entries(h1_t, c)), ACT.Copy)

        inv = {}
        for t in range(PACK):
            fetch_first(0, t)
        for t in range(PACK):
            tile = keep.tile([P, S], F32, name=f"y{t}")
            nc.vector.tensor_scalar(tile[:], y_ps[t][:], unit_t[:, t : t + 1], None, ALU.mult)
            y.append(tile)
        for h in range(2):
            mag = keep.tile([P, 2, S], F32, name=f"mag{h}")
            root = keep.tile([P, 2, S], F32, name=f"root{h}")
            for i in range(2):
                nc.scalar.activation(mag[:, i, :], ye_ps[2 * h + i][:], ACT.Abs)
            nc.scalar.activation(root[:], mag[:], ACT.Abs_reciprocal_sqrt, bias=0.7)
            for i in range(2):
                inv[2 * h + i] = keep.tile([P, S], F32, name=f"inv{2 * h + i}")
                nc.scalar.activation(inv[2 * h + i][:], root[:, i, :], ACT.Square)
        w3_bf = grouped_weight("w3")

        def add_note(c, t):
            if t == 0:
                sums[c] = keep.tile([P, PACK, CHUNKS[c]], F32, name=f"sum{c}", tag=f"sum{c}", align_bytes=64)
            nc.vector.tensor_tensor(sums[c][:, t, :], y[t][:].indirect(entries(nt_t, c)), first[c, t][:], ALU.add)

        def divide(c, t):
            if t == 0:
                hid[c] = keep.tile([P, PACK, CHUNKS[c]], F32, name=f"hid{c}", tag=f"hid{c}", align_bytes=64)
            if c in SCALAR_FETCHES:
                nc.scalar.activation(hid[c][:, t, :], inv[t][:].indirect(entries(h2_t, c)), ACT.Copy)
            else:
                nc.vector.tensor_tensor(hid[c][:, t, :], inv[t][:].indirect(entries(h2_t, c)), sums[c][:, t, :], ALU.mult)

        def by_column(ap):
            return ap.rearrange("p (c i) t -> p c t i", i=2)

        def by_slot(ap):
            return ap.rearrange("p t (c i) -> p c t i", i=2)

        def interleave(copy, dst, src):
            copy(by_column(dst), by_slot(src))

        last = len(CHUNKS) - 1
        groups = [(c, 0, CHUNKS[c]) for c in range(last)] + [(last, a, UNIT) for a in range(0, CHUNKS[last], UNIT)]

        def round_hid(k):
            c, a, width = groups[k]
            cols = slice(a, a + width)
            hid_bf[k] = keep.tile([P, width, PACK], BF16, name=f"hid_bf{k}", align_bytes=64)
            if c in SCALAR_FETCHES:
                nc.vector.tensor_tensor(
                    by_column(hid_bf[k][:]), by_slot(hid[c][:, :, cols]), by_slot(sums[c][:, :, cols]), ALU.mult
                )
            else:
                interleave(nc.vector.tensor_copy, hid_bf[k][:], hid[c][:, :, cols])

        out_plane = keep.tile([P, U], U8, name="out_plane", align_bytes=64)
        out_rows = out_0.rearrange("(p t) r -> p t r", t=PACK)
        out_words = out_1[0].rearrange("p c r -> p (c r)").bitcast(I32)
        w3_q = []

        def voices(k):
            c, a, width = groups[k]
            start = starts[c] + a
            codes = keep.tile([P, width], U32, name=f"hid_codes{k}", tag=f"hid{k + 2}", align_bytes=64)
            plane = keep.tile([P, width], U8, name=f"hid_plane{k}", align_bytes=64)
            nc.vector.quantize_mx(codes[:].bitcast(FP8X4), plane[:], hid_bf[k][:].rearrange("p n t -> p (n t)"))
            res[k] = keep.tile([P, PACK, width], F32, name=f"res{k}")
            if c == last:
                res_bf[k] = keep.tile([P, width, PACK], BF16, name=f"res_bf{k}", align_bytes=64)
            for u in range(width // UNIT):
                cols = slice(u * UNIT, (u + 1) * UNIT)
                g = start // UNIT + u
                bank = psum.tile([P, PACK, UNIT], F32, name=f"out_ps{g}", tag=f"bank{g}")
                for t in range(PACK):
                    product(bank[:, t, :], w3_q, t, codes[:, cols], plane[:, cols])
                if c == last:
                    interleave(nc.scalar.copy, res_bf[k][:, cols, :], bank[:])
                if k == len(groups) - 1:
                    nc.vector.tensor_copy(res[k][:, :, cols], bank[:])
                else:
                    nc.scalar.copy(res[k][:, :, cols], bank[:])
            nc.sync.dma_start(out_rows[:, :, start : start + width], res[k][:])

        def round_result(k):
            res_bf[k] = keep.tile([P, groups[k][2], PACK], BF16, name=f"res_bf{k}", tag=f"sum{k + 1}", align_bytes=64)
            interleave(nc.vector.tensor_copy, res_bf[k][:], res[k][:])

        out_codes = {}

        def hand_on(k):
            c, a, width = groups[k]
            if a == 0:
                out_codes[c] = keep.tile([P, CHUNKS[c]], I32, name=f"out_codes{c}", align_bytes=64)
            nc.vector.quantize_mx(
                out_codes[c][:, a : a + width].bitcast(FP8X4),
                out_plane[:, starts[c] + a : starts[c] + a + width],
                res_bf[k][:].rearrange("p n t -> p (n t)"),
            )
            if a + width == CHUNKS[c]:
                nc.sync.dma_start(out_words[:, starts[c] : starts[c] + CHUNKS[c]], out_codes[c][:])

        for c in range(len(CHUNKS)):
            add_note(c, 0)
            if c > 0:
                voices(c - 1)
            for t in range(1, PACK):
                add_note(c, t)
            if c == 0:
                for h in range(2):
                    round_weight(nc.vector.tensor_copy, w3_bf, w3_raw, h)
                for h in range(2):
                    w3_q.append(quantise_weight("w3", w3_bf, h))
            for t in range(PACK):
                divide(c, t)
            if c < last:
                for t in range(PACK):
                    fetch_first(c + 1, t)
            round_hid(c)
            if 0 < c < last:
                round_result(c - 1)
                hand_on(c - 1)
        for k in range(last + 1, len(groups)):
            round_hid(k)
        for k in range(last, len(groups)):
            voices(k)
        round_result(last - 1)
        for k in range(last - 1, len(groups)):
            hand_on(k)
        for q in range(4):
            queue = nc.sync if q % 2 else nc.scalar
            queue.dma_start(out_2[0, 4 * q : 4 * q + 4, :].bitcast(I32), out_plane[32 * q : 32 * q + 4, :].bitcast(I32))
